import numpy as np
import ml_dtypes


def mxq(x, axis, fmt="e4m3"):
    dtype, down = {"e4m3": (ml_dtypes.float8_e4m3fn, 7), "e5m2": (ml_dtypes.float8_e5m2, 14)}[fmt]
    v = np.moveaxis(np.asarray(x, np.float32).astype(ml_dtypes.bfloat16).astype(np.float64), axis, -1)
    blocks = v.reshape(v.shape[:-1] + (-1, 32))
    amax = np.abs(blocks).max(-1, keepdims=True)
    byte = np.maximum(np.where(amax > 0, np.frexp(amax)[1] - 1 + 127, 0) - down, 1)
    scale = np.exp2(byte - 127.0)
    codes = (blocks / scale).astype(np.float32).astype(dtype).astype(np.float64)
    return np.moveaxis((codes * scale).reshape(v.shape), -1, axis)


WIDE = False


def mx_kscale(k):
    if not WIDE:
        return np.ones(k)
    levels = np.array([10, -10, 5, -5, 0])
    if k % 512:
        return np.exp2(np.random.permutation(np.resize(levels, k // 32))).repeat(32)
    a = np.empty((k // 512, 16))
    for p in range(k // 512):
        a[p, :8] = np.random.permutation(np.resize(levels, 8))
        for g in range(8):
            far = levels[np.abs(levels - a[p, g]) >= 10]
            a[p, g + 8] = far[np.random.randint(len(far))]
    return np.exp2(a.ravel()).repeat(32)


def f64(x):
    return np.asarray(x).astype(np.float64)


def striped(idx):
    return np.tile(idx.reshape(-1, 16).T, (8, 1)).astype(np.uint16)


def unstriped(offs):
    return offs[:16].T.reshape(-1).astype(np.int64)


def striped8(idx):
    return np.concatenate([x.reshape(-1, 16).T for x in idx]).astype(np.uint16)


def runs(offs, k):
    lists = np.stack([offs[16 * r : 16 * r + 16].T.reshape(-1) for r in range(8)]).astype(np.int64)
    return lists[np.arange(k) % 512 // 64]


def pack_weight(w):
    k, n = w.shape
    w = f64(np.asarray(w, np.float32).astype(ml_dtypes.bfloat16)).reshape(k // 32, 32, n)
    amax = np.abs(w).max(1)
    byte = np.clip(np.where(amax > 0, np.frexp(amax)[1] - 1 + 127 - 7, 1), 1, 254)
    scaled = (w * np.exp2(127.0 - byte)[:, None, :]).reshape(k, n).astype(np.float32)
    words = np.ascontiguousarray(scaled.reshape(k // 512, 128, 4, n).transpose(0, 1, 3, 2)).astype(ml_dtypes.float8_e4m3fn).view(np.uint8)
    return words, np.ascontiguousarray(byte.astype(np.uint8).reshape(k // 512, 16, n))


def unpack_weight(words, scales):
    g, p, n, _ = words.shape
    vals = np.ascontiguousarray(words).view(ml_dtypes.float8_e4m3fn).astype(np.float64) * np.repeat(np.exp2(scales.astype(np.float64) - 127.0), 8, axis=1)[..., None]
    return vals.transpose(0, 1, 3, 2).reshape(g * 512, n)


K, T, S, N, G, H = 512, 2048, 512, 512, 2048, 512


def setup_inputs():
    n = np.random.standard_normal
    s = mx_kscale(K)[:, None]
    u = mx_kscale(S)
    packed_xT = pack_weight(n((K, T)) * s)
    packed_dT = pack_weight(n((K, G)) / s)
    return {
        "x_words": packed_xT[0],
        "x_scales": packed_xT[1],
        "d_words": packed_dT[0],
        "d_scales": packed_dT[1],
        "gn": (np.random.uniform(0.5, 1.5, (H, 1)) * u[:, None]).astype(np.float32),
        "w1": (n((H, N)) / np.sqrt(H) / u[:, None]).astype(np.float32),
        "offs": striped8(np.random.randint(0, T, (8, S))),
        "k1": striped8(np.random.randint(0, G, (8, H))),
        "n1": striped8(np.stack([np.random.permutation(S) for _ in range(8)])),
        "n2": striped(np.random.permutation(S)),
        "n3": striped(np.random.permutation(S)),
    }


def reference(x_words, x_scales, d_words, d_scales, gn, w1, offs, k1, n1, n2, n3):
    d_k1 = unpack_weight(d_words, d_scales)[np.arange(K)[:, None], runs(k1, K)]
    xq = unpack_weight(x_words, x_scales)[np.arange(K)[:, None], runs(offs, K)]
    h = 0.0625 * (d_k1.T @ xq)
    st = h - (h[np.arange(H)[:, None], runs(n1, H)])
    z = f64(gn) * (st - (0.5 * (st[np.arange(H)[:, None], runs(n1, H)])))
    h2 = mxq(f64(w1), 0, "e4m3").T @ mxq(z, 0, "e4m3")
    ex = np.exp(0.5 * h2)
    return (2.0 * ex) / (ex + ex[:, unstriped(n2)] + ex[:, unstriped(n3)])

@@ -1,0 +1,220 @@
+from contextlib import ExitStack
+
+import concourse.mybir as mybir
+
+K, T, S, N, G, H = 512, 2048, 512, 512, 2048, 512
+FLOPS = 2 * K * H * S + 2 * H * N * S
+
+F32 = mybir.dt.float32
+BF16 = mybir.dt.bfloat16
+U32 = mybir.dt.uint32
+I32 = mybir.dt.int32
+U16 = mybir.dt.uint16
+U8 = mybir.dt.uint8
+FP8X4 = mybir.dt.float8_e4m3fn_x4
+ACT = mybir.ActivationFunctionType
+ALU = mybir.AluOpType
+
+P = 128
+PACK = 4
+HALF = S // 2
+
+
+def tile_picked_hpqtwiceshare_none_p_kernel(
+    tc, x_words, x_scales, d_words, d_scales, gn, w1, offs, k1, n1, n2, n3, out
+):
+    nc = tc.nc
+    with ExitStack() as ctx:
+        sb = ctx.enter_context(tc.tile_pool(name="sb", bufs=1))
+        ps = ctx.enter_context(tc.psum_pool(name="ps", bufs=1))
+
+        def tile(name, shape, dtype):
+            return sb.tile(shape, dtype, name=name, align_bytes=64)
+
+        def entries(lst, half):
+            return lst[:, half * HALF // 16 : (half + 1) * HALF // 16]
+
+        def cols(half):
+            return slice(half * HALF, (half + 1) * HALF)
+
+        d_byte_tab = sb.tile([P, G], U8, name="d_byte_tab", tag="early0", align_bytes=64)
+        x_byte_tab = sb.tile([P, T], U8, name="x_byte_tab", tag="early1", align_bytes=64)
+        placed = tile("placed", [P, H + S], U8)
+        nc.vector.memset(d_byte_tab[:].bitcast(I32), 0)
+        nc.vector.memset(x_byte_tab[:].bitcast(I32), 0)
+        nc.vector.memset(placed[:].bitcast(I32), 0)
+
+        lists = {}
+
+        def load_list(name, src):
+            lists[name] = sb.tile([P, S // 16], U16, name="list_" + name)
+            nc.sync.dma_start(lists[name][:], src)
+
+        load_list("k1", k1)
+        load_list("offs", offs)
+        nc.scalar.dma_start(out=d_byte_tab[0:P:8, :].bitcast(I32), in_=d_scales[0].bitcast(I32))
+        nc.scalar.dma_start(out=x_byte_tab[0:P:8, :].bitcast(I32), in_=x_scales[0].bitcast(I32))
+        d_word_tab = tile("d_word_tab", [P, G], I32)
+        x_word_tab = tile("x_word_tab", [P, T], I32)
+        nc.sync.dma_start(out=d_word_tab[:], in_=d_words[0].rearrange("p c r -> p (c r)").bitcast(I32))
+        load_list("n1", n1)
+        load_list("n2", n2)
+        load_list("n3", n3)
+        nc.sync.dma_start(out=x_word_tab[:], in_=x_words[0].rearrange("p c r -> p (c r)").bitcast(I32))
+
+        gain = tile("gain", [P, PACK], F32)
+        nc.gpsimd.dma_start(out=gain[:], in_=gn.rearrange("(p t) o -> p (t o)", t=PACK))
+        h_scale = tile("h_scale", [P, PACK], F32)
+        nc.scalar.activation(out=h_scale[:], in_=gain[:], func=ACT.Copy, scale=0.0625)
+
+        picked_bytes = tile("picked_bytes", [P, H + S], U8)
+        nc.vector.tensor_copy(out=picked_bytes[:, 0:H], in_=d_byte_tab[:].indirect(lists["k1"][:]))
+        nc.vector.tensor_copy(out=picked_bytes[:, H : H + S], in_=x_byte_tab[:].indirect(lists["offs"][:]))
+        for a in range(4):
+            nc.scalar.dma_start(out=placed[a:P:32, :].bitcast(I32), in_=picked_bytes[8 * a : P : 32, :].bitcast(I32))
+
+        w_raw = []
+        for half in range(2):
+            w_half = sb.tile([P, PACK, HALF], F32, name="w_raw%d" % half, tag="early%d" % (1 - half), align_bytes=64)
+            nc.sync.dma_start(out=w_half[:], in_=w1.rearrange("(p t) m -> p t m", t=PACK)[:, :, cols(half)])
+            w_raw.append(w_half)
+
+        d_picked = tile("d_picked", [P, H], U32)
+        nc.vector.tensor_copy(out=d_picked[:], in_=d_word_tab[:].bitcast(U32).indirect(lists["k1"][:]))
+        d_codes = tile("d_codes", [P, H], U32)
+        nc.vector.tensor_copy(
+            out=d_codes[:].rearrange("p (t m) -> p m t", t=PACK),
+            in_=d_picked[:].rearrange("p (m t) -> p m t", t=PACK),
+        )
+        x_codes = tile("x_codes", [P, S], U32)
+        d_bytes = tile("d_bytes", [P, H], U8)
+        nc.vector.tensor_copy(out=x_codes[:, cols(0)], in_=x_word_tab[:].bitcast(U32).indirect(entries(lists["offs"], 0)))
+        nc.vector.tensor_copy(
+            out=d_bytes[:].rearrange("p (t m) -> p m t", t=PACK),
+            in_=placed[:, 0:H].rearrange("p (m t) -> p m t", t=PACK),
+        )
+        nc.vector.tensor_copy(out=x_codes[:, cols(1)], in_=x_word_tab[:].bitcast(U32).indirect(entries(lists["offs"], 1)))
+
+        def bank(index):
+            return ps.tile([P, S], F32, name="bank%d" % index)
+
+        def product(acc, lhs_codes, lhs_bytes, block, rhs_codes, rhs_bytes):
+            nc.tensor.matmul_mx(
+                out=acc,
+                lhsT=lhs_codes[:, block * P : (block + 1) * P].bitcast(FP8X4),
+                lhsT_scale=lhs_bytes[:, block * P : (block + 1) * P],
+                rhs=rhs_codes.bitcast(FP8X4),
+                rhs_scale=rhs_bytes,
+                start=True,
+                stop=True,
+            )
+
+        h_ps = {}
+        for half in range(2):
+            for t in range(PACK):
+                acc = bank(half * PACK + t)
+                product(acc[:, 0:HALF], d_codes, d_bytes, t, x_codes[:, cols(half)], placed[:, H + half * HALF : H + (half + 1) * HALF])
+                h_ps[t, half] = acc
+
+        w_codes = tile("w_codes", [P, N], U32)
+        w_bytes = tile("w_bytes", [P, N], U8)
+
+        def quantise(name, planes, codes, scale_bytes):
+            grouped = tile(name, [P, HALF * PACK], BF16)
+            nc.vector.tensor_copy(
+                out=grouped[:].rearrange("p (c i t) -> p c t i", i=4, t=PACK),
+                in_=planes[:].rearrange("p t (c i) -> p c t i", i=4),
+            )
+            nc.vector.quantize_mx(out=codes.bitcast(FP8X4), scales=scale_bytes, in_=grouped[:])
+
+        for half in range(2):
+            quantise("w_grouped%d" % half, w_raw[half], w_codes[:, cols(half)], w_bytes[:, cols(half)])
+
+        h_window, h_plain, st_window = {}, {}, {}
+
+        def h_out(t):
+            h_window[t] = tile("h_window%d" % t, [P, S], F32)
+            for half in range(2):
+                nc.scalar.activation(
+                    out=h_window[t][:, cols(half)], in_=h_ps[t, half][:, 0:HALF], func=ACT.Copy, scale=h_scale[:, t : t + 1]
+                )
+
+        def h_twin(t):
+            h_plain[t] = tile("h_plain%d" % t, [P, S], F32)
+            nc.sync.dma_start(out=h_plain[t][:], in_=h_window[t][:])
+
+        def st_fused(t):
+            st_window[t] = tile("st_window%d" % t, [P, S], F32)
+            for half in range(2):
+                nc.vector.tensor_tensor(
+                    st_window[t][:, cols(half)], h_window[t][:].indirect(entries(lists["n1"], half)), h_plain[t][:, cols(half)], ALU.subtract
+                )
+
+        def st_split(t):
+            st_window[t] = tile("st_window%d" % t, [P, S], F32)
+            for half in range(2):
+                fetched = tile("h_fetched%d_%d" % (t, half), [P, HALF], F32)
+                nc.scalar.activation(out=fetched[:], in_=h_window[t][:].indirect(entries(lists["n1"], half)), func=ACT.Copy)
+                nc.vector.scalar_tensor_tensor(
+                    out=st_window[t][:, cols(half)], in0=h_ps[t, half][:, 0:HALF], scalar=h_scale[:, t : t + 1], in1=fetched[:],
+                    op0=ALU.mult, op1=ALU.subtract,
+                )
+
+        for t in (0, 1):
+            h_out(t)
+            h_twin(t)
+        h_out(2)
+        st_split(2)
+        st_fused(0)
+        h_out(3)
+        st_fused(1)
+        st_split(3)
+
+        z_codes = tile("z_codes", [P, S], U32)
+        z_bytes = tile("z_bytes", [P, S], U8)
+        ex_window = [tile("ex_window%d" % b, [P, S], F32) for b in range(N // P)]
+        ex_plain = [tile("ex_plain%d" % b, [P, HALF], F32) for b in range(N // P)]
+        for half in range(2):
+            z_planes = tile("z_planes%d" % half, [P, PACK, HALF], BF16)
+            for t in (2, 0, 1, 3):
+                fetched = tile("st_fetched%d_%d" % (t, half), [P, HALF], F32)
+                nc.scalar.activation(out=fetched[:], in_=st_window[t][:].indirect(entries(lists["n1"], half)), func=ACT.Copy)
+                negated = t in (0, 1)
+                nc.vector.scalar_tensor_tensor(
+                    out=z_planes[:, t, :], in0=fetched[:], scalar=0.5 if negated else -0.5, in1=st_window[t][:, cols(half)],
+                    op0=ALU.mult, op1=ALU.subtract if negated else ALU.add,
+                )
+            quantise("z_grouped%d" % half, z_planes, z_codes[:, cols(half)], z_bytes[:, cols(half)])
+
+        for half in range(2):
+            for b in range(N // P):
+                acc = bank(half * PACK + b)
+                product(acc[:, 0:HALF], w_codes, w_bytes, b, z_codes[:, cols(half)], z_bytes[:, cols(half)])
+                nc.scalar.activation(out=ex_window[b][:, cols(half)], in_=acc[:, 0:HALF], func=ACT.Exp, scale=0.5)
+                if half == 0:
+                    nc.sync.dma_start(out=ex_plain[b][:], in_=ex_window[b][:, cols(0)])
+
+        def finish(b, half, den):
+            root = tile("root%d_%d" % (b, half), [P, HALF], F32)
+            nc.scalar.activation(out=root[:], in_=den[:], func=ACT.Abs_reciprocal_sqrt, scale=0.5)
+            inv = tile("inv%d_%d" % (b, half), [P, HALF], F32)
+            nc.scalar.activation(out=inv[:], in_=root[:], func=ACT.Square)
+            res = tile("res%d_%d" % (b, half), [P, HALF], F32)
+            nc.vector.tensor_tensor(res[:], inv[:], ex_window[b][:, cols(half)], ALU.mult)
+            nc.sync.dma_start(out=out[b * P : (b + 1) * P, cols(half)], in_=res[:])
+
+        second = {}
+        for b in range(N // P):
+            second[b] = tile("ex_n2_%d" % b, [P, HALF], F32)
+            nc.scalar.activation(out=second[b][:], in_=ex_window[b][:].indirect(entries(lists["n2"], 1)), func=ACT.Copy)
+            two = tile("two%d" % b, [P, HALF], F32)
+            nc.vector.tensor_tensor(two[:], ex_window[b][:].indirect(entries(lists["n2"], 0)), ex_plain[b][:], ALU.add)
+            den = tile("den%d_0" % b, [P, HALF], F32)
+            nc.vector.tensor_tensor(den[:], ex_window[b][:].indirect(entries(lists["n3"], 0)), two[:], ALU.add)
+            finish(b, 0, den)
+        for b in range(N // P):
+            others = tile("others%d" % b, [P, HALF], F32)
+            nc.vector.tensor_tensor(others[:], ex_window[b][:].indirect(entries(lists["n3"], 1)), second[b][:], ALU.add)
+            den = tile("den%d_1" % b, [P, HALF], F32)
+            nc.vector.tensor_tensor(den[:], others[:], ex_window[b][:, cols(1)], ALU.add)
+            finish(b, 1, den)

@@ -18,6 +18,11 @@ ALU = mybir.AluOpType
 P = 128
 PACK = 4
 HALF = S // 2
+SCALAR_FETCHED = (2, 3)
+VECTOR_TWINNED = ()
+Z_PIECES = (256, 256)
+SCALAR_INTERLEAVED = ()
+TWINNED_BLOCKS = (0, 1, 2)
 
 
 def tile_picked_hpqtwiceshare_none_p_kernel(
@@ -28,21 +33,20 @@ def tile_picked_hpqtwiceshare_none_p_kernel(
         sb = ctx.enter_context(tc.tile_pool(name="sb", bufs=1))
         ps = ctx.enter_context(tc.psum_pool(name="ps", bufs=1))
 
-        def tile(name, shape, dtype):
-            return sb.tile(shape, dtype, name=name, align_bytes=64)
+        def tile(name, shape, dtype, tag=None):
+            return sb.tile(shape, dtype, name=name, tag=tag or name, align_bytes=64)
 
-        def entries(lst, half):
-            return lst[:, half * HALF // 16 : (half + 1) * HALF // 16]
+        def entries(lst, span):
+            return lst[:, span.start // 16 : span.stop // 16]
 
         def cols(half):
             return slice(half * HALF, (half + 1) * HALF)
 
-        d_byte_tab = sb.tile([P, G], U8, name="d_byte_tab", tag="early0", align_bytes=64)
-        x_byte_tab = sb.tile([P, T], U8, name="x_byte_tab", tag="early1", align_bytes=64)
+        d_byte_tab = tile("d_byte_tab", [P, G], U8, tag="d_bytes_then_picked_words")
+        x_byte_tab = tile("x_byte_tab", [P, T], U8)
         placed = tile("placed", [P, H + S], U8)
-        nc.vector.memset(d_byte_tab[:].bitcast(I32), 0)
-        nc.vector.memset(x_byte_tab[:].bitcast(I32), 0)
-        nc.vector.memset(placed[:].bitcast(I32), 0)
+        for cleared in (d_byte_tab, x_byte_tab, placed):
+            nc.vector.memset(cleared[:].bitcast(I32), 0)
 
         lists = {}
 
@@ -54,18 +58,20 @@ def tile_picked_hpqtwiceshare_none_p_kernel(
         load_list("offs", offs)
         nc.scalar.dma_start(out=d_byte_tab[0:P:8, :].bitcast(I32), in_=d_scales[0].bitcast(I32))
         nc.scalar.dma_start(out=x_byte_tab[0:P:8, :].bitcast(I32), in_=x_scales[0].bitcast(I32))
-        d_word_tab = tile("d_word_tab", [P, G], I32)
-        x_word_tab = tile("x_word_tab", [P, T], I32)
+        d_word_tab = tile("d_word_tab", [P, G], I32, tag="d_words_then_w1")
         nc.sync.dma_start(out=d_word_tab[:], in_=d_words[0].rearrange("p c r -> p (c r)").bitcast(I32))
         load_list("n1", n1)
         load_list("n2", n2)
         load_list("n3", n3)
+        gain = tile("gain", [P, PACK], F32, tag="gain_then_x_words")
+        nc.scalar.dma_start(out=gain[:], in_=gn.rearrange("(p t) o -> p (t o)", t=PACK))
+        h_scale = tile("h_scale", [P, PACK], F32)
+        nc.vector.tensor_scalar(out=h_scale[:], in0=gain[:], scalar1=0.0625, scalar2=None, op0=ALU.mult)
+        x_word_tab = tile("x_word_tab", [P, T], I32, tag="gain_then_x_words")
         nc.sync.dma_start(out=x_word_tab[:], in_=x_words[0].rearrange("p c r -> p (c r)").bitcast(I32))
 
-        gain = tile("gain", [P, PACK], F32)
-        nc.gpsimd.dma_start(out=gain[:], in_=gn.rearrange("(p t) o -> p (t o)", t=PACK))
-        h_scale = tile("h_scale", [P, PACK], F32)
-        nc.scalar.activation(out=h_scale[:], in_=gain[:], func=ACT.Copy, scale=0.0625)
+        def deal(dst, src):
+            nc.vector.tensor_copy(out=dst.rearrange("p (t m) -> p m t", t=PACK), in_=src.rearrange("p (m t) -> p m t", t=PACK))
 
         picked_bytes = tile("picked_bytes", [P, H + S], U8)
         nc.vector.tensor_copy(out=picked_bytes[:, 0:H], in_=d_byte_tab[:].indirect(lists["k1"][:]))
@@ -73,27 +79,23 @@ def tile_picked_hpqtwiceshare_none_p_kernel(
         for a in range(4):
             nc.scalar.dma_start(out=placed[a:P:32, :].bitcast(I32), in_=picked_bytes[8 * a : P : 32, :].bitcast(I32))
 
-        w_raw = []
-        for half in range(2):
-            w_half = sb.tile([P, PACK, HALF], F32, name="w_raw%d" % half, tag="early%d" % (1 - half), align_bytes=64)
-            nc.sync.dma_start(out=w_half[:], in_=w1.rearrange("(p t) m -> p t m", t=PACK)[:, :, cols(half)])
-            w_raw.append(w_half)
-
-        d_picked = tile("d_picked", [P, H], U32)
+        d_picked = tile("d_picked", [P, H], U32, tag="d_bytes_then_picked_words")
         nc.vector.tensor_copy(out=d_picked[:], in_=d_word_tab[:].bitcast(U32).indirect(lists["k1"][:]))
-        d_codes = tile("d_codes", [P, H], U32)
-        nc.vector.tensor_copy(
-            out=d_codes[:].rearrange("p (t m) -> p m t", t=PACK),
-            in_=d_picked[:].rearrange("p (m t) -> p m t", t=PACK),
-        )
+        w_raw = tile("w_raw", [P, 2, PACK * HALF], F32, tag="d_words_then_w1")
+        for half in range(2):
+            nc.sync.dma_start(
+                out=w_raw[:, half, :].rearrange("p (t m) -> p t m", t=PACK),
+                in_=w1.rearrange("(p t) m -> p t m", t=PACK)[:, :, cols(half)],
+            )
+
         x_codes = tile("x_codes", [P, S], U32)
+        d_codes = tile("d_codes", [P, H], U32)
+        nc.vector.tensor_copy(out=x_codes[:, cols(0)], in_=x_word_tab[:].bitcast(U32).indirect(entries(lists["offs"], cols(0))))
+        deal(d_codes[:], d_picked[:])
+        nc.vector.tensor_copy(out=x_codes[:, cols(1)], in_=x_word_tab[:].bitcast(U32).indirect(entries(lists["offs"], cols(1))))
         d_bytes = tile("d_bytes", [P, H], U8)
-        nc.vector.tensor_copy(out=x_codes[:, cols(0)], in_=x_word_tab[:].bitcast(U32).indirect(entries(lists["offs"], 0)))
-        nc.vector.tensor_copy(
-            out=d_bytes[:].rearrange("p (t m) -> p m t", t=PACK),
-            in_=placed[:, 0:H].rearrange("p (m t) -> p m t", t=PACK),
-        )
-        nc.vector.tensor_copy(out=x_codes[:, cols(1)], in_=x_word_tab[:].bitcast(U32).indirect(entries(lists["offs"], 1)))
+        deal(d_bytes[:], placed[:, 0:H])
+        x_bytes = placed[:, H : H + S]
 
         def bank(index):
             return ps.tile([P, S], F32, name="bank%d" % index)
@@ -110,89 +112,109 @@ def tile_picked_hpqtwiceshare_none_p_kernel(
             )
 
         h_ps = {}
-        for half in range(2):
-            for t in range(PACK):
+        for t in range(PACK):
+            for half in range(2):
                 acc = bank(half * PACK + t)
-                product(acc[:, 0:HALF], d_codes, d_bytes, t, x_codes[:, cols(half)], placed[:, H + half * HALF : H + (half + 1) * HALF])
+                product(acc[:, 0:HALF], d_codes, d_bytes, t, x_codes[:, cols(half)], x_bytes[:, cols(half)])
                 h_ps[t, half] = acc
+
+        def quantise(name, planes, codes, scale_bytes, on_scalar=False):
+            width = planes.shape[2]
+            grouped = tile(name, [P, width * PACK], BF16)
+            dst = grouped[:].rearrange("p (c i t) -> p c t i", i=4, t=PACK)
+            src = planes.rearrange("p t (c i) -> p c t i", i=4)
+            if on_scalar:
+                nc.scalar.copy(out=dst, in_=src)
+            else:
+                nc.vector.tensor_copy(out=dst, in_=src)
+            nc.vector.quantize_mx(out=codes.bitcast(FP8X4), scales=scale_bytes, in_=grouped[:])
 
         w_codes = tile("w_codes", [P, N], U32)
         w_bytes = tile("w_bytes", [P, N], U8)
 
-        def quantise(name, planes, codes, scale_bytes):
-            grouped = tile(name, [P, HALF * PACK], BF16)
-            nc.vector.tensor_copy(
-                out=grouped[:].rearrange("p (c i t) -> p c t i", i=4, t=PACK),
-                in_=planes[:].rearrange("p t (c i) -> p c t i", i=4),
-            )
-            nc.vector.quantize_mx(out=codes.bitcast(FP8X4), scales=scale_bytes, in_=grouped[:])
+        def quantise_w(half):
+            quantise("w_grouped%d" % half, w_raw[:, half, :].rearrange("p (t m) -> p t m", t=PACK), w_codes[:, cols(half)], w_bytes[:, cols(half)])
 
-        for half in range(2):
-            quantise("w_grouped%d" % half, w_raw[half], w_codes[:, cols(half)], w_bytes[:, cols(half)])
-
-        h_window, h_plain, st_window = {}, {}, {}
+        h_window, h_twin, st_window = {}, {}, {}
 
         def h_out(t):
             h_window[t] = tile("h_window%d" % t, [P, S], F32)
             for half in range(2):
-                nc.scalar.activation(
-                    out=h_window[t][:, cols(half)], in_=h_ps[t, half][:, 0:HALF], func=ACT.Copy, scale=h_scale[:, t : t + 1]
-                )
+                nc.scalar.activation(out=h_window[t][:, cols(half)], in_=h_ps[t, half][:, 0:HALF], func=ACT.Copy, scale=h_scale[:, t : t + 1])
+            if t not in SCALAR_FETCHED:
+                h_twin[t] = tile("h_twin%d" % t, [P, S], F32)
+                if t in VECTOR_TWINNED:
+                    for half in range(2):
+                        nc.vector.tensor_scalar(out=h_twin[t][:, cols(half)], in0=h_ps[t, half][:, 0:HALF], scalar1=h_scale[:, t : t + 1], scalar2=None, op0=ALU.mult)
+                else:
+                    nc.sync.dma_start(out=h_twin[t][:], in_=h_window[t][:])
 
-        def h_twin(t):
-            h_plain[t] = tile("h_plain%d" % t, [P, S], F32)
-            nc.sync.dma_start(out=h_plain[t][:], in_=h_window[t][:])
-
-        def st_fused(t):
+        def first_lookup(t):
             st_window[t] = tile("st_window%d" % t, [P, S], F32)
             for half in range(2):
-                nc.vector.tensor_tensor(
-                    st_window[t][:, cols(half)], h_window[t][:].indirect(entries(lists["n1"], half)), h_plain[t][:, cols(half)], ALU.subtract
-                )
+                picked = h_window[t][:].indirect(entries(lists["n1"], cols(half)))
+                if t in SCALAR_FETCHED:
+                    fetched = tile("h_fetched%d_%d" % (t, half), [P, HALF], F32)
+                    nc.scalar.activation(out=fetched[:], in_=picked, func=ACT.Copy)
+                    nc.vector.scalar_tensor_tensor(
+                        out=st_window[t][:, cols(half)], in0=h_ps[t, half][:, 0:HALF], scalar=h_scale[:, t : t + 1], in1=fetched[:],
+                        op0=ALU.mult, op1=ALU.subtract,
+                    )
+                else:
+                    nc.vector.tensor_tensor(st_window[t][:, cols(half)], picked, h_twin[t][:, cols(half)], ALU.subtract)
 
-        def st_split(t):
-            st_window[t] = tile("st_window%d" % t, [P, S], F32)
-            for half in range(2):
-                fetched = tile("h_fetched%d_%d" % (t, half), [P, HALF], F32)
-                nc.scalar.activation(out=fetched[:], in_=h_window[t][:].indirect(entries(lists["n1"], half)), func=ACT.Copy)
-                nc.vector.scalar_tensor_tensor(
-                    out=st_window[t][:, cols(half)], in0=h_ps[t, half][:, 0:HALF], scalar=h_scale[:, t : t + 1], in1=fetched[:],
-                    op0=ALU.mult, op1=ALU.subtract,
-                )
-
-        for t in (0, 1):
-            h_out(t)
-            h_twin(t)
+        quantise_w(0)
+        quantise_w(1)
+        h_out(0)
+        h_out(1)
         h_out(2)
-        st_split(2)
-        st_fused(0)
+        first_lookup(2)
+        first_lookup(0)
         h_out(3)
-        st_fused(1)
-        st_split(3)
+        first_lookup(1)
+        first_lookup(3)
 
         z_codes = tile("z_codes", [P, S], U32)
         z_bytes = tile("z_bytes", [P, S], U8)
         ex_window = [tile("ex_window%d" % b, [P, S], F32) for b in range(N // P)]
-        ex_plain = [tile("ex_plain%d" % b, [P, HALF], F32) for b in range(N // P)]
-        for half in range(2):
-            z_planes = tile("z_planes%d" % half, [P, PACK, HALF], BF16)
+        ex_twin = {}
+        spans = [slice(sum(Z_PIECES[:k]), sum(Z_PIECES[: k + 1])) for k in range(len(Z_PIECES))]
+        for k, span in enumerate(spans):
+            width = Z_PIECES[k]
+            z_planes = tile("z_planes%d" % k, [P, PACK, width], BF16)
             for t in (2, 0, 1, 3):
-                fetched = tile("st_fetched%d_%d" % (t, half), [P, HALF], F32)
-                nc.scalar.activation(out=fetched[:], in_=st_window[t][:].indirect(entries(lists["n1"], half)), func=ACT.Copy)
-                negated = t in (0, 1)
+                fetched = tile("st_fetched%d_%d" % (t, k), [P, width], F32, tag="st_fetched%d" % t)
+                nc.scalar.activation(out=fetched[:], in_=st_window[t][:].indirect(entries(lists["n1"], span)), func=ACT.Copy)
+                plain = t in SCALAR_FETCHED
                 nc.vector.scalar_tensor_tensor(
-                    out=z_planes[:, t, :], in0=fetched[:], scalar=0.5 if negated else -0.5, in1=st_window[t][:, cols(half)],
-                    op0=ALU.mult, op1=ALU.subtract if negated else ALU.add,
+                    out=z_planes[:, t, :], in0=fetched[:], scalar=-0.5 if plain else 0.5, in1=st_window[t][:, span],
+                    op0=ALU.mult, op1=ALU.add if plain else ALU.subtract,
                 )
-            quantise("z_grouped%d" % half, z_planes, z_codes[:, cols(half)], z_bytes[:, cols(half)])
+            quantise("z_grouped%d" % k, z_planes[:], z_codes[:, span], z_bytes[:, span], on_scalar=k in SCALAR_INTERLEAVED)
 
-        for half in range(2):
+        for k, span in enumerate(spans):
+            width = Z_PIECES[k]
             for b in range(N // P):
-                acc = bank(half * PACK + b)
-                product(acc[:, 0:HALF], w_codes, w_bytes, b, z_codes[:, cols(half)], z_bytes[:, cols(half)])
-                nc.scalar.activation(out=ex_window[b][:, cols(half)], in_=acc[:, 0:HALF], func=ACT.Exp, scale=0.5)
-                if half == 0:
-                    nc.sync.dma_start(out=ex_plain[b][:], in_=ex_window[b][:, cols(0)])
+                acc = bank((k % 2) * PACK + b)
+                product(acc[:, 0:width], w_codes, w_bytes, b, z_codes[:, span], z_bytes[:, span])
+                nc.scalar.activation(out=ex_window[b][:, span], in_=acc[:, 0:width], func=ACT.Exp, scale=0.5)
+                if span.stop == HALF and b in TWINNED_BLOCKS:
+                    ex_twin[b] = tile("ex_twin%d" % b, [P, HALF], F32)
+                    nc.sync.dma_start(out=ex_twin[b][:], in_=ex_window[b][:, cols(0)])
+
+        def denominator(b, half):
+            span = cols(half)
+            den = tile("den%d_%d" % (b, half), [P, HALF], F32)
+            part = tile("part%d_%d" % (b, half), [P, HALF], F32)
+            if half == 0 and b in TWINNED_BLOCKS:
+                nc.vector.tensor_tensor(part[:], ex_window[b][:].indirect(entries(lists["n2"], span)), ex_twin[b][:], ALU.add)
+                nc.vector.tensor_tensor(den[:], ex_window[b][:].indirect(entries(lists["n3"], span)), part[:], ALU.add)
+            else:
+                fetched = tile("ex_fetched%d_%d" % (b, half), [P, HALF], F32)
+                nc.scalar.activation(out=fetched[:], in_=ex_window[b][:].indirect(entries(lists["n2"], span)), func=ACT.Copy)
+                nc.vector.tensor_tensor(part[:], ex_window[b][:].indirect(entries(lists["n3"], span)), fetched[:], ALU.add)
+                nc.vector.tensor_tensor(den[:], part[:], ex_window[b][:, span], ALU.add)
+            return den
 
         def finish(b, half, den):
             root = tile("root%d_%d" % (b, half), [P, HALF], F32)
@@ -203,18 +225,10 @@ def tile_picked_hpqtwiceshare_none_p_kernel(
             nc.vector.tensor_tensor(res[:], inv[:], ex_window[b][:, cols(half)], ALU.mult)
             nc.sync.dma_start(out=out[b * P : (b + 1) * P, cols(half)], in_=res[:])
 
-        second = {}
-        for b in range(N // P):
-            second[b] = tile("ex_n2_%d" % b, [P, HALF], F32)
-            nc.scalar.activation(out=second[b][:], in_=ex_window[b][:].indirect(entries(lists["n2"], 1)), func=ACT.Copy)
-            two = tile("two%d" % b, [P, HALF], F32)
-            nc.vector.tensor_tensor(two[:], ex_window[b][:].indirect(entries(lists["n2"], 0)), ex_plain[b][:], ALU.add)
-            den = tile("den%d_0" % b, [P, HALF], F32)
-            nc.vector.tensor_tensor(den[:], ex_window[b][:].indirect(entries(lists["n3"], 0)), two[:], ALU.add)
-            finish(b, 0, den)
-        for b in range(N // P):
-            others = tile("others%d" % b, [P, HALF], F32)
-            nc.vector.tensor_tensor(others[:], ex_window[b][:].indirect(entries(lists["n3"], 1)), second[b][:], ALU.add)
-            den = tile("den%d_1" % b, [P, HALF], F32)
-            nc.vector.tensor_tensor(den[:], others[:], ex_window[b][:, cols(1)], ALU.add)
-            finish(b, 1, den)
+        dens = {}
+        for half in range(2):
+            for b in range(N // P):
+                dens[b, half] = denominator(b, half)
+        for half in range(2):
+            for b in range(N // P):
+                finish(b, half, dens[b, half])

@@ -18,8 +18,9 @@ ALU = mybir.AluOpType
 P = 128
 PACK = 4
 HALF = S // 2
-SCALAR_FETCHED = (2, 3)
+SCALAR_FETCHED = ()
 VECTOR_TWINNED = ()
+VECTOR_COPIED = ()
 Z_PIECES = (256, 256)
 SCALAR_INTERLEAVED = ()
 TWINNED_BLOCKS = (0, 1, 2)
@@ -56,19 +57,20 @@ def tile_picked_hpqtwiceshare_none_p_kernel(
 
         load_list("k1", k1)
         load_list("offs", offs)
-        nc.scalar.dma_start(out=d_byte_tab[0:P:8, :].bitcast(I32), in_=d_scales[0].bitcast(I32))
-        nc.scalar.dma_start(out=x_byte_tab[0:P:8, :].bitcast(I32), in_=x_scales[0].bitcast(I32))
+        nc.sync.dma_start(out=d_byte_tab[0:P:8, :].bitcast(I32), in_=d_scales[0].bitcast(I32))
+        nc.sync.dma_start(out=x_byte_tab[0:P:8, :].bitcast(I32), in_=x_scales[0].bitcast(I32))
         d_word_tab = tile("d_word_tab", [P, G], I32, tag="d_words_then_w1")
-        nc.sync.dma_start(out=d_word_tab[:], in_=d_words[0].rearrange("p c r -> p (c r)").bitcast(I32))
         load_list("n1", n1)
         load_list("n2", n2)
         load_list("n3", n3)
-        gain = tile("gain", [P, PACK], F32, tag="gain_then_x_words")
-        nc.scalar.dma_start(out=gain[:], in_=gn.rearrange("(p t) o -> p (t o)", t=PACK))
+        nc.sync.dma_start(out=d_word_tab[:], in_=d_words[0].rearrange("p c r -> p (c r)").bitcast(I32))
+        x_word_tab = tile("x_word_tab", [P, T], I32)
+        nc.sync.dma_start(out=x_word_tab[:], in_=x_words[0].rearrange("p c r -> p (c r)").bitcast(I32))
+
+        gain = tile("gain", [P, PACK], F32)
+        nc.gpsimd.dma_start(out=gain[:], in_=gn.rearrange("(p t) o -> p (t o)", t=PACK))
         h_scale = tile("h_scale", [P, PACK], F32)
         nc.vector.tensor_scalar(out=h_scale[:], in0=gain[:], scalar1=0.0625, scalar2=None, op0=ALU.mult)
-        x_word_tab = tile("x_word_tab", [P, T], I32, tag="gain_then_x_words")
-        nc.sync.dma_start(out=x_word_tab[:], in_=x_words[0].rearrange("p c r -> p (c r)").bitcast(I32))
 
         def deal(dst, src):
             nc.vector.tensor_copy(out=dst.rearrange("p (t m) -> p m t", t=PACK), in_=src.rearrange("p (m t) -> p m t", t=PACK))
@@ -133,19 +135,25 @@ def tile_picked_hpqtwiceshare_none_p_kernel(
         w_bytes = tile("w_bytes", [P, N], U8)
 
         def quantise_w(half):
-            quantise("w_grouped%d" % half, w_raw[:, half, :].rearrange("p (t m) -> p t m", t=PACK), w_codes[:, cols(half)], w_bytes[:, cols(half)])
+            quantise("w_grouped%d" % half, w_raw[:, half, :].rearrange("p (t m) -> p t m", t=PACK), w_codes[:, cols(half)], w_bytes[:, cols(half)], on_scalar=half in ())
 
         h_window, h_twin, st_window = {}, {}, {}
 
         def h_out(t):
             h_window[t] = tile("h_window%d" % t, [P, S], F32)
             for half in range(2):
-                nc.scalar.activation(out=h_window[t][:, cols(half)], in_=h_ps[t, half][:, 0:HALF], func=ACT.Copy, scale=h_scale[:, t : t + 1])
+                if t in VECTOR_COPIED:
+                    nc.vector.tensor_scalar(out=h_window[t][:, cols(half)], in0=h_ps[t, half][:, 0:HALF], scalar1=h_scale[:, t : t + 1], scalar2=None, op0=ALU.mult)
+                else:
+                    nc.scalar.activation(out=h_window[t][:, cols(half)], in_=h_ps[t, half][:, 0:HALF], func=ACT.Copy, scale=h_scale[:, t : t + 1])
             if t not in SCALAR_FETCHED:
                 h_twin[t] = tile("h_twin%d" % t, [P, S], F32)
                 if t in VECTOR_TWINNED:
                     for half in range(2):
                         nc.vector.tensor_scalar(out=h_twin[t][:, cols(half)], in0=h_ps[t, half][:, 0:HALF], scalar1=h_scale[:, t : t + 1], scalar2=None, op0=ALU.mult)
+                elif t in (0,1,2,3):
+                    for half in range(2):
+                        nc.scalar.activation(out=h_twin[t][:, cols(half)], in_=h_ps[t, half][:, 0:HALF], func=ACT.Copy, scale=h_scale[:, t : t + 1])
                 else:
                     nc.sync.dma_start(out=h_twin[t][:], in_=h_window[t][:])
 
@@ -163,15 +171,15 @@ def tile_picked_hpqtwiceshare_none_p_kernel(
                 else:
                     nc.vector.tensor_tensor(st_window[t][:, cols(half)], picked, h_twin[t][:, cols(half)], ALU.subtract)
 
-        quantise_w(0)
-        quantise_w(1)
         h_out(0)
         h_out(1)
         h_out(2)
-        first_lookup(2)
-        first_lookup(0)
         h_out(3)
+        quantise_w(0)
+        quantise_w(1)
+        first_lookup(0)
         first_lookup(1)
+        first_lookup(2)
         first_lookup(3)
 
         z_codes = tile("z_codes", [P, S], U32)
@@ -182,7 +190,7 @@ def tile_picked_hpqtwiceshare_none_p_kernel(
         for k, span in enumerate(spans):
             width = Z_PIECES[k]
             z_planes = tile("z_planes%d" % k, [P, PACK, width], BF16)
-            for t in (2, 0, 1, 3):
+            for t in (0,1,2,3):
                 fetched = tile("st_fetched%d_%d" % (t, k), [P, width], F32, tag="st_fetched%d" % t)
                 nc.scalar.activation(out=fetched[:], in_=st_window[t][:].indirect(entries(lists["n1"], span)), func=ACT.Copy)
                 plain = t in SCALAR_FETCHED
@@ -198,9 +206,12 @@ def tile_picked_hpqtwiceshare_none_p_kernel(
                 acc = bank((k % 2) * PACK + b)
                 product(acc[:, 0:width], w_codes, w_bytes, b, z_codes[:, span], z_bytes[:, span])
                 nc.scalar.activation(out=ex_window[b][:, span], in_=acc[:, 0:width], func=ACT.Exp, scale=0.5)
-                if span.stop == HALF and b in TWINNED_BLOCKS:
+                if k == 0 and b in TWINNED_BLOCKS:
                     ex_twin[b] = tile("ex_twin%d" % b, [P, HALF], F32)
-                    nc.sync.dma_start(out=ex_twin[b][:], in_=ex_window[b][:, cols(0)])
+                    if b in (0,1,2):
+                        nc.scalar.activation(out=ex_twin[b][:], in_=acc[:, 0:width], func=ACT.Exp, scale=0.5)
+                    else:
+                        nc.sync.dma_start(out=ex_twin[b][:], in_=ex_window[b][:, cols(0)])
 
         def denominator(b, half):
             span = cols(half)

@@ -68,9 +68,9 @@ def tile_picked_hpqtwiceshare_none_p_kernel(
         nc.sync.dma_start(out=x_word_tab[:], in_=x_words[0].rearrange("p c r -> p (c r)").bitcast(I32))
 
         gain = tile("gain", [P, PACK], F32)
-        nc.gpsimd.dma_start(out=gain[:], in_=gn.rearrange("(p t) o -> p (t o)", t=PACK))
+        nc.sync.dma_start(out=gain[:], in_=gn.rearrange("(p t) o -> p (t o)", t=PACK))
         h_scale = tile("h_scale", [P, PACK], F32)
-        nc.vector.tensor_scalar(out=h_scale[:], in0=gain[:], scalar1=0.0625, scalar2=None, op0=ALU.mult)
+        nc.scalar.activation(out=h_scale[:], in_=gain[:], func=ACT.Copy, scale=0.0625)
 
         def deal(dst, src):
             nc.vector.tensor_copy(out=dst.rearrange("p (t m) -> p m t", t=PACK), in_=src.rearrange("p (m t) -> p m t", t=PACK))

from contextlib import ExitStack

import concourse.mybir as mybir

K, T, S, N, G, H = 512, 2048, 512, 512, 2048, 512
FLOPS = 2 * K * H * S + 2 * H * N * S

F32 = mybir.dt.float32
BF16 = mybir.dt.bfloat16
U32 = mybir.dt.uint32
I32 = mybir.dt.int32
U16 = mybir.dt.uint16
U8 = mybir.dt.uint8
FP8X4 = mybir.dt.float8_e4m3fn_x4
ACT = mybir.ActivationFunctionType
ALU = mybir.AluOpType

P = 128
PACK = 4
HALF = S // 2
SCALAR_FETCHED = ()
VECTOR_TWINNED = ()
VECTOR_COPIED = ()
Z_PIECES = (256, 256)
SCALAR_INTERLEAVED = ()
TWINNED_BLOCKS = (0, 1, 2)


def tile_picked_hpqtwiceshare_none_p_kernel(
    tc, x_words, x_scales, d_words, d_scales, gn, w1, offs, k1, n1, n2, n3, out
):
    nc = tc.nc
    with ExitStack() as ctx:
        sb = ctx.enter_context(tc.tile_pool(name="sb", bufs=1))
        ps = ctx.enter_context(tc.psum_pool(name="ps", bufs=1))

        def tile(name, shape, dtype, tag=None):
            return sb.tile(shape, dtype, name=name, tag=tag or name, align_bytes=64)

        def entries(lst, span):
            return lst[:, span.start // 16 : span.stop // 16]

        def cols(half):
            return slice(half * HALF, (half + 1) * HALF)

        d_byte_tab = tile("d_byte_tab", [P, G], U8, tag="d_bytes_then_picked_words")
        x_byte_tab = tile("x_byte_tab", [P, T], U8)
        placed = tile("placed", [P, H + S], U8)
        for cleared in (d_byte_tab, x_byte_tab, placed):
            nc.vector.memset(cleared[:].bitcast(I32), 0)

        lists = {}

        def load_list(name, src):
            lists[name] = sb.tile([P, S // 16], U16, name="list_" + name)
            nc.sync.dma_start(lists[name][:], src)

        load_list("k1", k1)
        load_list("offs", offs)
        nc.sync.dma_start(out=d_byte_tab[0:P:8, :].bitcast(I32), in_=d_scales[0].bitcast(I32))
        nc.sync.dma_start(out=x_byte_tab[0:P:8, :].bitcast(I32), in_=x_scales[0].bitcast(I32))
        d_word_tab = tile("d_word_tab", [P, G], I32, tag="d_words_then_w1")
        load_list("n1", n1)
        load_list("n2", n2)
        load_list("n3", n3)
        nc.sync.dma_start(out=d_word_tab[:], in_=d_words[0].rearrange("p c r -> p (c r)").bitcast(I32))
        x_word_tab = tile("x_word_tab", [P, T], I32)
        nc.sync.dma_start(out=x_word_tab[:], in_=x_words[0].rearrange("p c r -> p (c r)").bitcast(I32))

        gain = tile("gain", [P, PACK], F32)
        nc.sync.dma_start(out=gain[:], in_=gn.rearrange("(p t) o -> p (t o)", t=PACK))
        h_scale = tile("h_scale", [P, PACK], F32)
        nc.scalar.activation(out=h_scale[:], in_=gain[:], func=ACT.Copy, scale=0.0625)

        def deal(dst, src):
            nc.vector.tensor_copy(out=dst.rearrange("p (t m) -> p m t", t=PACK), in_=src.rearrange("p (m t) -> p m t", t=PACK))

        picked_bytes = tile("picked_bytes", [P, H + S], U8)
        nc.vector.tensor_copy(out=picked_bytes[:, 0:H], in_=d_byte_tab[:].indirect(lists["k1"][:]))
        nc.vector.tensor_copy(out=picked_bytes[:, H : H + S], in_=x_byte_tab[:].indirect(lists["offs"][:]))
        for a in range(4):
            nc.scalar.dma_start(out=placed[a:P:32, :].bitcast(I32), in_=picked_bytes[8 * a : P : 32, :].bitcast(I32))

        d_picked = tile("d_picked", [P, H], U32, tag="d_bytes_then_picked_words")
        nc.vector.tensor_copy(out=d_picked[:], in_=d_word_tab[:].bitcast(U32).indirect(lists["k1"][:]))
        w_raw = tile("w_raw", [P, 2, PACK * HALF], F32, tag="d_words_then_w1")
        for half in range(2):
            nc.sync.dma_start(
                out=w_raw[:, half, :].rearrange("p (t m) -> p t m", t=PACK),
                in_=w1.rearrange("(p t) m -> p t m", t=PACK)[:, :, cols(half)],
            )

        x_codes = tile("x_codes", [P, S], U32)
        d_codes = tile("d_codes", [P, H], U32)
        nc.vector.tensor_copy(out=x_codes[:, cols(0)], in_=x_word_tab[:].bitcast(U32).indirect(entries(lists["offs"], cols(0))))
        deal(d_codes[:], d_picked[:])
        nc.vector.tensor_copy(out=x_codes[:, cols(1)], in_=x_word_tab[:].bitcast(U32).indirect(entries(lists["offs"], cols(1))))
        d_bytes = tile("d_bytes", [P, H], U8)
        deal(d_bytes[:], placed[:, 0:H])
        x_bytes = placed[:, H : H + S]

        def bank(index):
            return ps.tile([P, S], F32, name="bank%d" % index)

        def product(acc, lhs_codes, lhs_bytes, block, rhs_codes, rhs_bytes):
            nc.tensor.matmul_mx(
                out=acc,
                lhsT=lhs_codes[:, block * P : (block + 1) * P].bitcast(FP8X4),
                lhsT_scale=lhs_bytes[:, block * P : (block + 1) * P],
                rhs=rhs_codes.bitcast(FP8X4),
                rhs_scale=rhs_bytes,
                start=True,
                stop=True,
            )

        h_ps = {}
        for t in range(PACK):
            for half in range(2):
                acc = bank(half * PACK + t)
                product(acc[:, 0:HALF], d_codes, d_bytes, t, x_codes[:, cols(half)], x_bytes[:, cols(half)])
                h_ps[t, half] = acc

        def quantise(name, planes, codes, scale_bytes, on_scalar=False):
            width = planes.shape[2]
            grouped = tile(name, [P, width * PACK], BF16)
            dst = grouped[:].rearrange("p (c i t) -> p c t i", i=4, t=PACK)
            src = planes.rearrange("p t (c i) -> p c t i", i=4)
            if on_scalar:
                nc.scalar.copy(out=dst, in_=src)
            else:
                nc.vector.tensor_copy(out=dst, in_=src)
            nc.vector.quantize_mx(out=codes.bitcast(FP8X4), scales=scale_bytes, in_=grouped[:])

        w_codes = tile("w_codes", [P, N], U32)
        w_bytes = tile("w_bytes", [P, N], U8)

        def quantise_w(half):
            quantise("w_grouped%d" % half, w_raw[:, half, :].rearrange("p (t m) -> p t m", t=PACK), w_codes[:, cols(half)], w_bytes[:, cols(half)], on_scalar=half in ())

        h_window, h_twin, st_window = {}, {}, {}

        def h_out(t):
            h_window[t] = tile("h_window%d" % t, [P, S], F32)
            for half in range(2):
                if t in VECTOR_COPIED:
                    nc.vector.tensor_scalar(out=h_window[t][:, cols(half)], in0=h_ps[t, half][:, 0:HALF], scalar1=h_scale[:, t : t + 1], scalar2=None, op0=ALU.mult)
                else:
                    nc.scalar.activation(out=h_window[t][:, cols(half)], in_=h_ps[t, half][:, 0:HALF], func=ACT.Copy, scale=h_scale[:, t : t + 1])
            if t not in SCALAR_FETCHED:
                h_twin[t] = tile("h_twin%d" % t, [P, S], F32)
                if t in VECTOR_TWINNED:
                    for half in range(2):
                        nc.vector.tensor_scalar(out=h_twin[t][:, cols(half)], in0=h_ps[t, half][:, 0:HALF], scalar1=h_scale[:, t : t + 1], scalar2=None, op0=ALU.mult)
                elif t in (0,1,2,3):
                    for half in range(2):
                        nc.scalar.activation(out=h_twin[t][:, cols(half)], in_=h_ps[t, half][:, 0:HALF], func=ACT.Copy, scale=h_scale[:, t : t + 1])
                else:
                    nc.sync.dma_start(out=h_twin[t][:], in_=h_window[t][:])

        def first_lookup(t):
            st_window[t] = tile("st_window%d" % t, [P, S], F32)
            for half in range(2):
                picked = h_window[t][:].indirect(entries(lists["n1"], cols(half)))
                if t in SCALAR_FETCHED:
                    fetched = tile("h_fetched%d_%d" % (t, half), [P, HALF], F32)
                    nc.scalar.activation(out=fetched[:], in_=picked, func=ACT.Copy)
                    nc.vector.scalar_tensor_tensor(
                        out=st_window[t][:, cols(half)], in0=h_ps[t, half][:, 0:HALF], scalar=h_scale[:, t : t + 1], in1=fetched[:],
                        op0=ALU.mult, op1=ALU.subtract,
                    )
                else:
                    nc.vector.tensor_tensor(st_window[t][:, cols(half)], picked, h_twin[t][:, cols(half)], ALU.subtract)

        h_out(0)
        h_out(1)
        h_out(2)
        h_out(3)
        quantise_w(0)
        quantise_w(1)
        first_lookup(0)
        first_lookup(1)
        first_lookup(2)
        first_lookup(3)

        z_codes = tile("z_codes", [P, S], U32)
        z_bytes = tile("z_bytes", [P, S], U8)
        ex_window = [tile("ex_window%d" % b, [P, S], F32) for b in range(N // P)]
        ex_twin = {}
        spans = [slice(sum(Z_PIECES[:k]), sum(Z_PIECES[: k + 1])) for k in range(len(Z_PIECES))]
        for k, span in enumerate(spans):
            width = Z_PIECES[k]
            z_planes = tile("z_planes%d" % k, [P, PACK, width], BF16)
            for t in (0,1,2,3):
                fetched = tile("st_fetched%d_%d" % (t, k), [P, width], F32, tag="st_fetched%d" % t)
                nc.scalar.activation(out=fetched[:], in_=st_window[t][:].indirect(entries(lists["n1"], span)), func=ACT.Copy)
                plain = t in SCALAR_FETCHED
                nc.vector.scalar_tensor_tensor(
                    out=z_planes[:, t, :], in0=fetched[:], scalar=-0.5 if plain else 0.5, in1=st_window[t][:, span],
                    op0=ALU.mult, op1=ALU.add if plain else ALU.subtract,
                )
            quantise("z_grouped%d" % k, z_planes[:], z_codes[:, span], z_bytes[:, span], on_scalar=k in SCALAR_INTERLEAVED)

        for k, span in enumerate(spans):
            width = Z_PIECES[k]
            for b in range(N // P):
                acc = bank((k % 2) * PACK + b)
                product(acc[:, 0:width], w_codes, w_bytes, b, z_codes[:, span], z_bytes[:, span])
                nc.scalar.activation(out=ex_window[b][:, span], in_=acc[:, 0:width], func=ACT.Exp, scale=0.5)
                if k == 0 and b in TWINNED_BLOCKS:
                    ex_twin[b] = tile("ex_twin%d" % b, [P, HALF], F32)
                    if b in (0,1,2):
                        nc.scalar.activation(out=ex_twin[b][:], in_=acc[:, 0:width], func=ACT.Exp, scale=0.5)
                    else:
                        nc.sync.dma_start(out=ex_twin[b][:], in_=ex_window[b][:, cols(0)])

        def denominator(b, half):
            span = cols(half)
            den = tile("den%d_%d" % (b, half), [P, HALF], F32)
            part = tile("part%d_%d" % (b, half), [P, HALF], F32)
            if half == 0 and b in TWINNED_BLOCKS:
                nc.vector.tensor_tensor(part[:], ex_window[b][:].indirect(entries(lists["n2"], span)), ex_twin[b][:], ALU.add)
                nc.vector.tensor_tensor(den[:], ex_window[b][:].indirect(entries(lists["n3"], span)), part[:], ALU.add)
            else:
                fetched = tile("ex_fetched%d_%d" % (b, half), [P, HALF], F32)
                nc.scalar.activation(out=fetched[:], in_=ex_window[b][:].indirect(entries(lists["n2"], span)), func=ACT.Copy)
                nc.vector.tensor_tensor(part[:], ex_window[b][:].indirect(entries(lists["n3"], span)), fetched[:], ALU.add)
                nc.vector.tensor_tensor(den[:], part[:], ex_window[b][:, span], ALU.add)
            return den

        def finish(b, half, den):
            root = tile("root%d_%d" % (b, half), [P, HALF], F32)
            nc.scalar.activation(out=root[:], in_=den[:], func=ACT.Abs_reciprocal_sqrt, scale=0.5)
            inv = tile("inv%d_%d" % (b, half), [P, HALF], F32)
            nc.scalar.activation(out=inv[:], in_=root[:], func=ACT.Square)
            res = tile("res%d_%d" % (b, half), [P, HALF], F32)
            nc.vector.tensor_tensor(res[:], inv[:], ex_window[b][:, cols(half)], ALU.mult)
            nc.sync.dma_start(out=out[b * P : (b + 1) * P, cols(half)], in_=res[:])

        dens = {}
        for half in range(2):
            for b in range(N // P):
                dens[b, half] = denominator(b, half)
        for half in range(2):
            for b in range(N // P):
                finish(b, half, dens[b, half])
